import numpy as np
import ml_dtypes


def mxq(x, axis, fmt="e4m3"):
    dtype, down = {"e4m3": (ml_dtypes.float8_e4m3fn, 7), "e5m2": (ml_dtypes.float8_e5m2, 14)}[fmt]
    v = np.moveaxis(np.asarray(x, np.float32).astype(ml_dtypes.bfloat16).astype(np.float64), axis, -1)
    blocks = v.reshape(v.shape[:-1] + (-1, 32))
    amax = np.abs(blocks).max(-1, keepdims=True)
    byte = np.maximum(np.where(amax > 0, np.frexp(amax)[1] - 1 + 127, 0) - down, 1)
    scale = np.exp2(byte - 127.0)
    codes = (blocks / scale).astype(np.float32).astype(dtype).astype(np.float64)
    return np.moveaxis((codes * scale).reshape(v.shape), -1, axis)


WIDE = False


def mx_kscale(k):
    if not WIDE:
        return np.ones(k)
    levels = np.array([10, -10, 5, -5, 0])
    if k % 512:
        return np.exp2(np.random.permutation(np.resize(levels, k // 32))).repeat(32)
    a = np.empty((k // 512, 16))
    for p in range(k // 512):
        a[p, :8] = np.random.permutation(np.resize(levels, 8))
        for g in range(8):
            far = levels[np.abs(levels - a[p, g]) >= 10]
            a[p, g + 8] = far[np.random.randint(len(far))]
    return np.exp2(a.ravel()).repeat(32)


def f64(x):
    return np.asarray(x).astype(np.float64)


def striped(idx):
    return np.tile(idx.reshape(-1, 16).T, (8, 1)).astype(np.uint16)


def unstriped(offs):
    return offs[:16].T.reshape(-1).astype(np.int64)


E2M1 = np.array([0.0, 0.5, 1.0, 1.5, 2.0, 3.0, 4.0, 6.0, -0.0, -0.5, -1.0, -1.5, -2.0, -3.0, -4.0, -6.0])


def pack_weight(w, fmt):
    k, n = w.shape
    w = f64(np.asarray(w, np.float32).astype(ml_dtypes.bfloat16)).reshape(k // 32, 32, n)
    amax = np.abs(w).max(1)
    if fmt == "e4m3":
        byte = np.frexp(amax)[1] - 1 + 127 - 7
    else:
        mant, ex = np.frexp(amax / 6.0)
        byte = np.where(mant > 0.5, ex, ex - 1) + 127
    byte = np.clip(np.where(amax > 0, byte, 1), 1, 254)
    scaled = (w * np.exp2(127.0 - byte)[:, None, :]).reshape(k, n).astype(np.float32)
    by_word = np.ascontiguousarray(scaled.reshape(k // 512, 128, 4, n).transpose(0, 1, 3, 2))
    if fmt == "e4m3":
        words = by_word.astype(ml_dtypes.float8_e4m3fn).view(np.uint8)
    else:
        c = by_word.astype(ml_dtypes.float4_e2m1fn).view(np.uint8) & 0xF
        words = (c[..., 0::2] | (c[..., 1::2] << 4)).reshape(k // 512, 128, 2 * n)
    return np.ascontiguousarray(words), np.ascontiguousarray(byte.astype(np.uint8).reshape(k // 512, 16, n))


def unpack_weight(words, scales, fmt):
    g, _, n = scales.shape
    words = np.ascontiguousarray(words).reshape(g, 128, n, -1)
    if fmt == "e4m3":
        vals = words.view(ml_dtypes.float8_e4m3fn).astype(np.float64)
    else:
        nib = np.empty((g, 128, n, 4), np.uint8)
        nib[..., 0::2] = words & 0xF
        nib[..., 1::2] = words >> 4
        vals = E2M1[nib]
    vals = vals * np.repeat(np.exp2(scales.astype(np.float64) - 127.0), 8, axis=1)[..., None]
    return vals.transpose(0, 1, 3, 2).reshape(g * 512, n)


def gelu(v):
    return 0.5 * v * (1.0 + np.tanh(np.sqrt(2.0 / np.pi) * (v + 0.044715 * v**3)))


K, M, H, N, T, S, P, T2 = 512, 1024, 1024, 384, 2048, 1024, 512, 2048

def setup_inputs():
    n = np.random.standard_normal
    s, s2, u = mx_kscale(K)[:, None], mx_kscale(M)[:, None], mx_kscale(H)[:, None]
    tab_words, tab_scales = pack_weight(n((K, T)) * s, "e4m3")
    tab2_words, tab2_scales = pack_weight(n((M, T)) * s2, "e4m3")
    w2_words, w2_scales = pack_weight(1.3 * n((M, H)) / np.sqrt(M) / s2, "e2m1")
    w3_words, w3_scales = pack_weight(1.2 * n((H, N)) / np.sqrt(H) / u, "e2m1")
    d2_words, d2_scales = pack_weight(0.7 * n((M, N)) / np.sqrt(M) / s2, "e4m3")
    perm = np.random.permutation(T2)
    return {"tab_words": tab_words, "tab_scales": tab_scales, "tab2_words": tab2_words, "tab2_scales": tab2_scales,
            "offs": striped(np.random.permutation(T)[:S]), "offs2": striped(np.random.permutation(T)[:P]),
            "pos1": striped(np.random.permutation(S)[:P]),
            "offs3": striped(perm[:S]), "offs4": striped(perm[S:S + P]),
            "w1": (1.3 * n((K, H)) / np.sqrt(K) / s).astype(np.float32),
            "d1": (0.7 * n((K, N)) / np.sqrt(K) / s).astype(np.float32),
            "w2_words": w2_words, "w2_scales": w2_scales, "d2_words": d2_words, "d2_scales": d2_scales,
            "w3_words": w3_words, "w3_scales": w3_scales,
            "w4": (n((H, N)) / np.sqrt(H) / u).astype(np.float32),
            "g1": (np.exp(0.4 * n(H)) * u[:, 0]).astype(np.float32), "g2": (np.exp(0.4 * n(H)) * u[:, 0]).astype(np.float32),
            "wg1": np.exp(0.3 * n((128, S))).astype(np.float32), "wg2": np.exp(0.3 * n((128, P))).astype(np.float32),
            "page1": n((N, T2)).astype(np.float32)}

def reference(tab_words, tab_scales, tab2_words, tab2_scales, offs, offs2, pos1, offs3, offs4, w1, d1,
              w2_words, w2_scales, d2_words, d2_scales, w3_words, w3_scales, w4, g1, g2, wg1, wg2, page1):
    v = unpack_weight(tab_words, tab_scales, "e4m3")[:, unstriped(offs)]
    v2 = unpack_weight(tab2_words, tab2_scales, "e4m3")[:, unstriped(offs2)]
    h1 = mxq(f64(w1), 0, "e4m3").T @ v
    h2 = unpack_weight(w2_words, w2_scales, "e2m1").T @ v2
    z1 = f64(g1)[:, None] * (0.5 * h1 * (1.0 + np.tanh(np.sqrt(2.0 / np.pi) * (h1 + 0.044715 * h1 ** 3))))
    z2 = f64(g2)[:, None] * np.minimum(h2, h1[:, unstriped(pos1)])
    y1 = unpack_weight(w3_words, w3_scales, "e2m1").T @ mxq(z1, 0, "e4m3") + mxq(f64(d1), 0, "e4m3").T @ v
    y2 = mxq(f64(w4), 0, "e4m3").T @ mxq(z2, 0, "e4m3") + unpack_weight(d2_words, d2_scales, "e4m3").T @ v2
    out = f64(page1).copy()
    out[:, unstriped(offs3)] = np.tile(f64(wg1), (N // 128, 1)) * y1
    out[:, unstriped(offs4)] = np.tile(f64(wg2), (N // 128, 1)) * y2
    return out

@@ -1,0 +1,293 @@
+from contextlib import ExitStack
+
+import concourse.mybir as mybir
+
+K, M, H, N, T, S, E = 512, 1024, 1024, 384, 2048, 1024, 512
+FLOPS = 4160749568
+
+F32 = mybir.dt.float32
+BF16 = mybir.dt.bfloat16
+I32 = mybir.dt.int32
+U32 = mybir.dt.uint32
+U16 = mybir.dt.uint16
+U8 = mybir.dt.uint8
+FP8X4 = mybir.dt.float8_e4m3fn_x4
+FP4X4 = mybir.dt.float4_e2m1fn_x4
+ACT = mybir.ActivationFunctionType
+ALU = mybir.AluOpType
+
+P = 128
+
+
+def tile_list_vol_surface_features_kernel(
+    tc, tab_words, tab_scales, tab2_words, tab2_scales, offs, offs2, pos1, offs3, offs4, w1, d1,
+    w2_words, w2_scales, d2_words, d2_scales, w3_words, w3_scales, w4, g1, g2, wg1, wg2, page1, out,
+):
+    nc = tc.nc
+    with ExitStack() as ctx:
+        keep = ctx.enter_context(tc.tile_pool(name="keep", bufs=1))
+        ring = ctx.enter_context(tc.tile_pool(name="ring", bufs=2))
+        psum = ctx.enter_context(tc.psum_pool(name="psum", bufs=1))
+
+        def held(shape, dtype, name):
+            return keep.tile(shape, dtype, name=name, align_bytes=64)
+
+        def load_list(src, name):
+            t = keep.tile(list(src.shape), U16, name=name)
+            nc.sync.dma_start(t[:], src)
+            return t
+
+        def zeroed(width, name, engine):
+            t = held([P, width], U8, name)
+            engine.memset(t[:].bitcast(I32), 0)
+            return t
+
+        def load_packed_scales(t, src, queue):
+            passes = src.shape[0]
+            for q in range(4):
+                queue.dma_start(
+                    t[32 * q : 32 * q + 4 * passes, :].bitcast(I32), src[:, 4 * q : 4 * q + 4, :].bitcast(I32)
+                )
+
+        def load_scales(t, src):
+            for q in range(4):
+                nc.sync.dma_start(
+                    t[32 * q : 32 * q + 4, :].bitcast(I32).rearrange("r (a c) -> r a c", a=2),
+                    src[:, 4 * q : 4 * q + 4, :].bitcast(I32).rearrange("a r c -> r a c"),
+                )
+
+        def load_words(src, name):
+            t = ring.tile([P, T], U32, name=name, tag="wide", bufs=3, align_bytes=64)
+            nc.sync.dma_start(t[:].bitcast(I32), src.rearrange("p t i -> p (t i)").bitcast(I32))
+            return t
+
+        def load_rows(src, name, tag):
+            t = ring.tile([P, 4, src.shape[1]], F32, name=name, tag=tag)
+            nc.sync.dma_start(t[:], src.rearrange("(p j) c -> p j c", j=4))
+            return t
+
+        def raise_second_plane(dst, src):
+            for q in range(4):
+                nc.sync.dma_start(dst[32 * q : 32 * q + 4, :].bitcast(I32), src[32 * q + 4 : 32 * q + 8, :].bitcast(I32))
+
+        def copy_on(engine, dst, src):
+            if engine is nc.scalar:
+                nc.scalar.copy(dst, src)
+            else:
+                engine.tensor_copy(dst, src)
+
+        def interleave(engine, dst, src):
+            copy_on(engine, dst.rearrange("p (c i) t -> p c t i", i=4), src.rearrange("p t (c i) -> p c t i", i=4))
+
+        def staged(cols, name):
+            return ring.tile([P, cols, 4], BF16, name=name, tag="staged", bufs=3, align_bytes=64)
+
+        def quantize(codes, scales, src):
+            nc.vector.quantize_mx(out=codes.bitcast(FP8X4), scales=scales, in_=src.rearrange("p c t -> p (c t)"))
+
+        tab2_sc = zeroed(T, "tab2_sc", nc.gpsimd)
+        w2_sc_raw = zeroed(2 * H, "w2_sc_raw", nc.gpsimd)
+        v2_sc1 = zeroed(E, "v2_sc1", nc.gpsimd)
+        w3_sc = zeroed(2 * N, "w3_sc", nc.gpsimd)
+        d2_sc = zeroed(N, "d2_sc", nc.gpsimd)
+        idx = load_list(offs, "idx")
+        tab_sc = held([P, T], U8, "tab_sc")
+        for q in range(4):
+            nc.sync.dma_start(
+                tab_sc[32 * q : 32 * (q + 1), :].bitcast(I32),
+                tab_scales[:, 4 * q : 4 * q + 4, :].bitcast(I32).broadcast_to([8, 4, T // 4]),
+            )
+        tab_w = load_words(tab_words[0], "tab_w")
+        w1_raw = [load_rows(w1[:, 0:256], "w1_raw0", "raw_a")]
+        w1_raw.append(load_rows(w1[:, 256:512], "w1_raw1", "raw_a"))
+        idx2 = load_list(offs2, "idx2")
+        load_packed_scales(tab2_sc, tab2_scales, nc.sync)
+        w1_raw.append(load_rows(w1[:, 512:768], "w1_raw2", "raw_b"))
+        w1_raw.append(load_rows(w1[:, 768:1024], "w1_raw3", "raw_b"))
+        central = load_list(pos1, "central")
+        tab2_w = [load_words(tab2_words[0], "tab2_w0")]
+        load_scales(w2_sc_raw, w2_scales)
+        w2_raw = ring.tile([P, 2, 2 * H], U8, name="w2_raw", tag="packed", bufs=1, align_bytes=64)
+        nc.sync.dma_start(w2_raw[:].bitcast(I32), w2_words.rearrange("a p c -> p a c").bitcast(I32))
+        tab2_w.append(load_words(tab2_words[1], "tab2_w1"))
+
+        v_sc = held([P, S], U8, "v_sc")
+        nc.vector.tensor_copy(v_sc[:], tab_sc[:].indirect(idx[:]))
+        v_w = held([P, S], U32, "v_w")
+        w1_q = held([P, H], U32, "w1_q")
+        w1_sc = held([P, H], U8, "w1_sc")
+        h1 = [held([P, 4, S], F32, "h1_%d" % b) for b in range(2)]
+        picked = [held([P, 4, E], F32, "picked%d" % b) for b in range(2)]
+
+        def quantize_w1(b):
+            st = staged(512, "w1_st")
+            for u in range(2):
+                nc.scalar.copy(
+                    st[:].rearrange("p (t m) j -> p m j t", t=4)[:, 64 * u : 64 * (u + 1)],
+                    w1_raw[2 * b + u][:].rearrange("p j (m t) -> p m j t", t=4),
+                )
+            quantize(w1_q[:, 512 * b : 512 * (b + 1)], w1_sc[:, 512 * b : 512 * (b + 1)], st[:])
+
+        nc.vector.tensor_copy(v_w[:], tab_w[:].indirect(idx[:]))
+        quantize_w1(0)
+        v2_sc = held([P, E], U8, "v2_sc")
+        nc.vector.tensor_copy(v2_sc[:], tab2_sc[:].indirect(idx2[:]))
+        raise_second_plane(v2_sc1, v2_sc)
+        quantize_w1(1)
+        for b in range(2):
+            for t in range(4):
+                rows = slice(512 * b + P * t, 512 * b + P * (t + 1))
+                for half in range(2):
+                    cols = slice(512 * half, 512 * (half + 1))
+                    bank = psum.tile([P, 512], F32, name="h1_bank", tag="h_bank", bufs=4)
+                    nc.tensor.matmul_mx(
+                        out=bank[:], lhsT=w1_q[:, rows].bitcast(FP8X4), lhsT_scale=w1_sc[:, rows],
+                        rhs=v_w[:, cols].bitcast(FP8X4), rhs_scale=v_sc[:, cols], start=True, stop=True,
+                    )
+                    nc.scalar.copy(h1[b][:, t, cols], bank[:])
+                nc.vector.tensor_copy(picked[b][:, t, :], h1[b][:, t, :].indirect(central[:]))
+
+        v2_w = held([P, 2, E], U32, "v2_w")
+        w2_w = held([P, 2, 2 * H], U8, "w2_w")
+        w2_sc = held([P, 2 * H], U8, "w2_sc")
+        nc.vector.tensor_copy(v2_w[:, 0, :], tab2_w[0][:].indirect(idx2[:]))
+        nc.vector.tensor_copy(
+            w2_sc[:].rearrange("p (b t m) -> p b t m", t=4, m=P), w2_sc_raw[:].rearrange("p (b m t) -> p b t m", t=4, m=P)
+        )
+        nc.vector.tensor_copy(
+            w2_w[:].rearrange("p a c -> p (a c)").bitcast(U16).rearrange("p (b t m) -> p b t m", t=4, m=P),
+            w2_raw[:].rearrange("p a c -> p (a c)").bitcast(U16).rearrange("p (b m t) -> p b t m", t=4, m=P),
+        )
+        nc.vector.tensor_copy(v2_w[:, 1, :], tab2_w[1][:].indirect(idx2[:]))
+        for b in range(2):
+            for t in range(4):
+                r0 = 512 * b + P * t
+                bank = psum.tile([P, E], F32, name="h2_bank", tag="h_bank", bufs=4)
+                for a in range(2):
+                    nc.tensor.matmul_mx(
+                        out=bank[:], lhsT=w2_w[:, a, 2 * r0 : 2 * (r0 + P)].bitcast(FP4X4),
+                        lhsT_scale=w2_sc[:, H * a + r0 : H * a + r0 + P],
+                        rhs=v2_w[:, a, :].bitcast(FP8X4), rhs_scale=(v2_sc, v2_sc1)[a][:], start=(a == 0), stop=(a == 1),
+                    )
+                nc.vector.tensor_tensor(picked[b][:, t, :], bank[:], picked[b][:, t, :], ALU.min)
+
+        gain1 = held([P, 2, 4], F32, "gain1")
+        nc.sync.dma_start(gain1[:], g1.rearrange("(b p t) -> p b t", b=2, t=4))
+        gain2 = held([P, 2, 4], F32, "gain2")
+        nc.sync.dma_start(gain2[:], g2.rearrange("(b p t) -> p b t", b=2, t=4))
+        d1_raw = load_rows(d1, "d1_raw", "raw_a")
+        w3_w = held([P, 2, 2 * N], U8, "w3_w")
+        nc.sync.dma_start(w3_w[:].bitcast(I32), w3_words.rearrange("a p c -> p a c").bitcast(I32))
+        load_scales(w3_sc, w3_scales)
+        w4_raw = [load_rows(w4[512 * b : 512 * (b + 1), :], "w4_raw%d" % b, "raw_b") for b in range(2)]
+        slots1 = load_list(offs3, "slots1")
+        factor1 = held([P, S], F32, "factor1")
+        nc.sync.dma_start(factor1[:], wg1)
+        pages = []
+        for n in range(3):
+            page = ring.tile([P, T], F32, name="page%d" % n, tag="page", bufs=3, align_bytes=64)
+            nc.sync.dma_start(page[:], page1[P * n : P * (n + 1), :])
+            pages.append(page)
+        load_packed_scales(d2_sc, d2_scales, nc.sync)
+        d2_w = held([P, 2, N], U32, "d2_w")
+        nc.sync.dma_start(d2_w[:].bitcast(I32), d2_words.rearrange("a p c i -> p a (c i)").bitcast(I32))
+        slots2 = load_list(offs4, "slots2")
+        factor2 = held([P, E], F32, "factor2")
+        nc.sync.dma_start(factor2[:], wg2)
+
+        def gain_and_interleave(src, gain, b, dst, engine):
+            rounded = ring.tile([P, 4, src.shape[2]], BF16, name="rounded", align_bytes=64)
+            for t in range(4):
+                nc.scalar.activation(rounded[:, t, :], src[:, t, :], ACT.Copy, scale=gain[:, b, t : t + 1])
+            interleave(engine, dst, rounded[:])
+
+        def z_tiles(width):
+            codes = ring.tile([P, 2 * width], U32, name="z_q", tag="z_q", align_bytes=64)
+            scales = ring.tile([P, 2 * width], U8, name="z_sc", tag="z_sc", align_bytes=64)
+            return codes, scales
+
+        def make_z1(j0, width, engine):
+            st = staged(2 * width, "z1_st")
+            for b in range(2):
+                act = ring.tile([P, 4, width], F32, name="act")
+                nc.scalar.activation(act[:], h1[b][:, :, j0 : j0 + width], ACT.Gelu_apprx_tanh)
+                gain_and_interleave(act[:], gain1, b, st[:, b * width : (b + 1) * width, :], engine[b])
+            codes, scales = z_tiles(width)
+            quantize(codes[:], scales[:], st[:])
+            return codes, scales
+
+        def make_z2(engine):
+            st = staged(2 * E, "z2_st")
+            for b in range(2):
+                gain_and_interleave(picked[b][:], gain2, b, st[:, b * E : (b + 1) * E, :], engine[b])
+            codes, scales = z_tiles(E)
+            quantize(codes[:], scales[:], st[:])
+            return codes, scales
+
+        def place(n, width, passes, slots, factor, last):
+            bank = psum.tile([P, width], F32, name="y_bank", tag="y_bank", bufs=4)
+            for i, (lhs, lhs_sc, rhs, rhs_sc) in enumerate(passes):
+                nc.tensor.matmul_mx(
+                    out=bank[:], lhsT=lhs, lhsT_scale=lhs_sc, rhs=rhs, rhs_scale=rhs_sc,
+                    start=(i == 0), stop=(i == len(passes) - 1),
+                )
+            y = ring.tile([P, width], F32, name="y", tag="y", bufs=4)
+            nc.scalar.copy(y[:], bank[:])
+            nc.vector.tensor_tensor(pages[n][:].indirect(slots), y[:], factor, ALU.mult)
+            if last:
+                nc.sync.dma_start(out[P * n : P * (n + 1), :], pages[n][:])
+
+        def place_y1(z, j0, width, last=False):
+            cols = slice(j0, j0 + width)
+            for n in range(3):
+                ns = slice(P * n, P * (n + 1))
+                passes = [(d1_q[:, ns].bitcast(FP8X4), d1_sc[:, ns], v_w[:, cols].bitcast(FP8X4), v_sc[:, cols])]
+                for b in range(2):
+                    zs = slice(b * width, (b + 1) * width)
+                    passes.append((
+                        w3_w[:, b, 2 * P * n : 2 * P * (n + 1)].bitcast(FP4X4), w3_sc[:, N * b + P * n : N * b + P * (n + 1)],
+                        z[0][:, zs].bitcast(FP8X4), z[1][:, zs],
+                    ))
+                place(n, width, passes, slots1[:, j0 // 16 : (j0 + width) // 16], factor1[:, cols], last)
+
+        def place_y2(z, last=False):
+            for n in range(3):
+                ns = slice(P * n, P * (n + 1))
+                passes = []
+                for a in range(2):
+                    passes.append((d2_w[:, a, ns].bitcast(FP8X4), d2_sc[4 * a : P, ns], v2_w[:, a, :].bitcast(FP8X4), v2_sc[4 * a : P, :]))
+                for b in range(2):
+                    ws = slice(N * b + P * n, N * b + P * (n + 1))
+                    zs = slice(b * E, (b + 1) * E)
+                    passes.append((w4_q[:, ws].bitcast(FP8X4), w4_sc[:, ws], z[0][:, zs].bitcast(FP8X4), z[1][:, zs]))
+                place(n, E, passes, slots2[:], factor2[:], last)
+
+        d1_q = held([P, N], U32, "d1_q")
+        d1_sc = held([P, N], U8, "d1_sc")
+        w4_q = held([P, 2 * N], U32, "w4_q")
+        w4_sc = held([P, 2 * N], U8, "w4_sc")
+
+        def quantize_d1(engine):
+            st = staged(N, "d1_st")
+            interleave(engine, st[:], d1_raw[:])
+            quantize(d1_q[:], d1_sc[:], st[:])
+
+        def quantize_w4(engine):
+            st = staged(2 * N, "w4_st")
+            for b in range(2):
+                interleave(engine, st[:, N * b : N * (b + 1), :], w4_raw[b][:])
+                quantize(w4_q[:, N * b : N * (b + 1)], w4_sc[:, N * b : N * (b + 1)], st[:, N * b : N * (b + 1), :])
+
+        ss, vv, sv, vs = (nc.scalar, nc.scalar), (nc.vector, nc.vector), (nc.scalar, nc.vector), (nc.vector, nc.scalar)
+        za = make_z1(0, 256, ss)
+        quantize_d1(nc.scalar)
+        quantize_w4(nc.vector)
+        z2 = make_z2(vv)
+        place_y1(za, 0, 256)
+        zb = make_z1(256, 256, ss)
+        place_y2(z2)
+        zc = make_z1(512, 256, ss)
+        place_y1(zb, 256, 256)
+        zd = make_z1(768, 256, ss)
+        place_y1(zc, 512, 256)
+        place_y1(zd, 768, 256, last=True)

@@ -42,13 +42,6 @@ def tile_list_vol_surface_features_kernel(
             engine.memset(t[:].bitcast(I32), 0)
             return t
 
-        def load_packed_scales(t, src, queue):
-            passes = src.shape[0]
-            for q in range(4):
-                queue.dma_start(
-                    t[32 * q : 32 * q + 4 * passes, :].bitcast(I32), src[:, 4 * q : 4 * q + 4, :].bitcast(I32)
-                )
-
         def load_scales(t, src):
             for q in range(4):
                 nc.sync.dma_start(
@@ -61,8 +54,8 @@ def tile_list_vol_surface_features_kernel(
             nc.sync.dma_start(t[:].bitcast(I32), src.rearrange("p t i -> p (t i)").bitcast(I32))
             return t
 
-        def load_rows(src, name, tag):
-            t = ring.tile([P, 4, src.shape[1]], F32, name=name, tag=tag)
+        def load_rows(src, name, tag, bufs=2):
+            t = ring.tile([P, 4, src.shape[1]], F32, name=name, tag=tag, bufs=bufs)
             nc.sync.dma_start(t[:], src.rearrange("(p j) c -> p j c", j=4))
             return t
 
@@ -79,17 +72,21 @@ def tile_list_vol_surface_features_kernel(
         def interleave(engine, dst, src):
             copy_on(engine, dst.rearrange("p (c i) t -> p c t i", i=4), src.rearrange("p t (c i) -> p c t i", i=4))
 
-        def staged(cols, name):
-            return ring.tile([P, cols, 4], BF16, name=name, tag="staged", bufs=3, align_bytes=64)
+        fetched = [held([P, 4, E], F32, "fetch%d_st" % b) for b in range(2)]
+        stage = [f[:].rearrange("p t c -> p (t c)").bitcast(BF16).rearrange("p (c t) -> p c t", t=4) for f in fetched]
+        banks = [psum.tile([P, 512], F32, name="bank%d" % i) for i in range(8)]
 
         def quantize(codes, scales, src):
             nc.vector.quantize_mx(out=codes.bitcast(FP8X4), scales=scales, in_=src.rearrange("p c t -> p (c t)"))
 
-        tab2_sc = zeroed(T, "tab2_sc", nc.gpsimd)
-        w2_sc_raw = zeroed(2 * H, "w2_sc_raw", nc.gpsimd)
-        v2_sc1 = zeroed(E, "v2_sc1", nc.gpsimd)
+        warm = held([P, 1], F32, "warm")
+        nc.gpsimd.memset(warm[:], 0.0)
+        warmed = held([P, 1], F32, "warmed")
+        nc.scalar.activation(warmed[:], warm[:], ACT.Gelu_apprx_tanh)
+        w2_sc_raw = zeroed(2 * H, "w2_sc_raw", nc.vector)
+        tab2_sc = zeroed(2 * T, "tab2_sc", nc.vector)
         w3_sc = zeroed(2 * N, "w3_sc", nc.gpsimd)
-        d2_sc = zeroed(N, "d2_sc", nc.gpsimd)
+        d2_sc = zeroed(2 * N, "d2_sc", nc.gpsimd)
         idx = load_list(offs, "idx")
         tab_sc = held([P, T], U8, "tab_sc")
         for q in range(4):
@@ -100,57 +97,57 @@ def tile_list_vol_surface_features_kernel(
         tab_w = load_words(tab_words[0], "tab_w")
         w1_raw = [load_rows(w1[:, 0:256], "w1_raw0", "raw_a")]
         w1_raw.append(load_rows(w1[:, 256:512], "w1_raw1", "raw_a"))
-        idx2 = load_list(offs2, "idx2")
-        load_packed_scales(tab2_sc, tab2_scales, nc.sync)
-        w1_raw.append(load_rows(w1[:, 512:768], "w1_raw2", "raw_b"))
-        w1_raw.append(load_rows(w1[:, 768:1024], "w1_raw3", "raw_b"))
         central = load_list(pos1, "central")
-        tab2_w = [load_words(tab2_words[0], "tab2_w0")]
+        w1_raw.append(load_rows(w1[:, 512:768], "w1_raw2", "first_rows", 1))
         load_scales(w2_sc_raw, w2_scales)
-        w2_raw = ring.tile([P, 2, 2 * H], U8, name="w2_raw", tag="packed", bufs=1, align_bytes=64)
+        w2_raw = held([P, 2, 2 * H], U8, "w2_raw")
         nc.sync.dma_start(w2_raw[:].bitcast(I32), w2_words.rearrange("a p c -> p a c").bitcast(I32))
-        tab2_w.append(load_words(tab2_words[1], "tab2_w1"))
+        w1_raw.append(load_rows(w1[:, 768:1024], "w1_raw3", "raw_b", 1))
+        idx2 = load_list(offs2, "idx2")
+        load_scales(tab2_sc, tab2_scales)
+        tab2_w = [load_words(tab2_words[a], "tab2_w%d" % a) for a in range(2)]
 
         v_sc = held([P, S], U8, "v_sc")
         nc.vector.tensor_copy(v_sc[:], tab_sc[:].indirect(idx[:]))
         v_w = held([P, S], U32, "v_w")
-        w1_q = held([P, H], U32, "w1_q")
-        w1_sc = held([P, H], U8, "w1_sc")
-        h1 = [held([P, 4, S], F32, "h1_%d" % b) for b in range(2)]
+        w1_q = [ring.tile([P, 512], U32, name="w1_q%d" % b, tag="codes%d" % b, bufs=1, align_bytes=64) for b in range(2)]
+        w1_sc = [ring.tile([P, 512], U8, name="w1_sc%d" % b, tag="plane%d" % b, bufs=1, align_bytes=64) for b in range(2)]
+        h1 = [ring.tile([P, 2, S], F32, name="h1_0", tag="first_rows", bufs=1)]
+        h1 = h1 + [held([P, 2, S], F32, "h1_%d" % i) for i in range(1, 4)]
         picked = [held([P, 4, E], F32, "picked%d" % b) for b in range(2)]
 
         def quantize_w1(b):
-            st = staged(512, "w1_st")
+            st = stage[b][:, 0:512, :]
             for u in range(2):
                 nc.scalar.copy(
-                    st[:].rearrange("p (t m) j -> p m j t", t=4)[:, 64 * u : 64 * (u + 1)],
+                    st.rearrange("p (t m) j -> p m j t", t=4)[:, 64 * u : 64 * (u + 1)],
                     w1_raw[2 * b + u][:].rearrange("p j (m t) -> p m j t", t=4),
                 )
-            quantize(w1_q[:, 512 * b : 512 * (b + 1)], w1_sc[:, 512 * b : 512 * (b + 1)], st[:])
+            quantize(w1_q[b][:], w1_sc[b][:], st)
 
         nc.vector.tensor_copy(v_w[:], tab_w[:].indirect(idx[:]))
         quantize_w1(0)
-        v2_sc = held([P, E], U8, "v2_sc")
-        nc.vector.tensor_copy(v2_sc[:], tab2_sc[:].indirect(idx2[:]))
-        raise_second_plane(v2_sc1, v2_sc)
         quantize_w1(1)
         for b in range(2):
             for t in range(4):
-                rows = slice(512 * b + P * t, 512 * b + P * (t + 1))
                 for half in range(2):
                     cols = slice(512 * half, 512 * (half + 1))
-                    bank = psum.tile([P, 512], F32, name="h1_bank", tag="h_bank", bufs=4)
+                    bank = banks[(2 * t + half) % 4]
                     nc.tensor.matmul_mx(
-                        out=bank[:], lhsT=w1_q[:, rows].bitcast(FP8X4), lhsT_scale=w1_sc[:, rows],
+                        out=bank[:], lhsT=w1_q[b][:, P * t : P * (t + 1)].bitcast(FP8X4), lhsT_scale=w1_sc[b][:, P * t : P * (t + 1)],
                         rhs=v_w[:, cols].bitcast(FP8X4), rhs_scale=v_sc[:, cols], start=True, stop=True,
                     )
-                    nc.scalar.copy(h1[b][:, t, cols], bank[:])
-                nc.vector.tensor_copy(picked[b][:, t, :], h1[b][:, t, :].indirect(central[:]))
+                    nc.scalar.copy(h1[2 * b + t // 2][:, t % 2, cols], bank[:])
+                nc.vector.tensor_copy(fetched[b][:, t, :], h1[2 * b + t // 2][:, t % 2, :].indirect(central[:]))
 
-        v2_w = held([P, 2, E], U32, "v2_w")
-        w2_w = held([P, 2, 2 * H], U8, "w2_w")
+        v2_w = [ring.tile([P, E], U32, name="v2_w%d" % a, tag="codes%d" % a, bufs=1, align_bytes=64) for a in range(2)]
+        w2_w = ring.tile([P, 2, 2 * H], U8, name="w2_w", tag="dealt", bufs=1, align_bytes=64)
         w2_sc = held([P, 2 * H], U8, "w2_sc")
-        nc.vector.tensor_copy(v2_w[:, 0, :], tab2_w[0][:].indirect(idx2[:]))
+        v2_planes = ring.tile([P, 2, E], U8, name="v2_planes", tag="plane0", bufs=1, align_bytes=64)
+        v2_sc = [v2_planes[:, a, :] for a in range(2)]
+        for a in range(2):
+            nc.vector.tensor_copy(v2_sc[a], tab2_sc[:, T * a : T * (a + 1)].indirect(idx2[:]))
+        nc.vector.tensor_copy(v2_w[0][:], tab2_w[0][:].indirect(idx2[:]))
         nc.vector.tensor_copy(
             w2_sc[:].rearrange("p (b t m) -> p b t m", t=4, m=P), w2_sc_raw[:].rearrange("p (b m t) -> p b t m", t=4, m=P)
         )
@@ -158,18 +155,18 @@ def tile_list_vol_surface_features_kernel(
             w2_w[:].rearrange("p a c -> p (a c)").bitcast(U16).rearrange("p (b t m) -> p b t m", t=4, m=P),
             w2_raw[:].rearrange("p a c -> p (a c)").bitcast(U16).rearrange("p (b m t) -> p b t m", t=4, m=P),
         )
-        nc.vector.tensor_copy(v2_w[:, 1, :], tab2_w[1][:].indirect(idx2[:]))
+        nc.vector.tensor_copy(v2_w[1][:], tab2_w[1][:].indirect(idx2[:]))
         for b in range(2):
             for t in range(4):
                 r0 = 512 * b + P * t
-                bank = psum.tile([P, E], F32, name="h2_bank", tag="h_bank", bufs=4)
+                bank = banks[t]
                 for a in range(2):
                     nc.tensor.matmul_mx(
                         out=bank[:], lhsT=w2_w[:, a, 2 * r0 : 2 * (r0 + P)].bitcast(FP4X4),
                         lhsT_scale=w2_sc[:, H * a + r0 : H * a + r0 + P],
-                        rhs=v2_w[:, a, :].bitcast(FP8X4), rhs_scale=(v2_sc, v2_sc1)[a][:], start=(a == 0), stop=(a == 1),
+                        rhs=v2_w[a][:].bitcast(FP8X4), rhs_scale=v2_sc[a], start=(a == 0), stop=(a == 1),
                     )
-                nc.vector.tensor_tensor(picked[b][:, t, :], bank[:], picked[b][:, t, :], ALU.min)
+                nc.vector.tensor_tensor(picked[b][:, t, :], bank[:], fetched[b][:, t, :], ALU.min)
 
         gain1 = held([P, 2, 4], F32, "gain1")
         nc.sync.dma_start(gain1[:], g1.rearrange("(b p t) -> p b t", b=2, t=4))
@@ -179,7 +176,7 @@ def tile_list_vol_surface_features_kernel(
         w3_w = held([P, 2, 2 * N], U8, "w3_w")
         nc.sync.dma_start(w3_w[:].bitcast(I32), w3_words.rearrange("a p c -> p a c").bitcast(I32))
         load_scales(w3_sc, w3_scales)
-        w4_raw = [load_rows(w4[512 * b : 512 * (b + 1), :], "w4_raw%d" % b, "raw_b") for b in range(2)]
+        w4_raw = [load_rows(w4[512 * b : 512 * (b + 1), :], "w4_raw%d" % b, ("raw_a", "raw_b")[b], 2 - b) for b in range(2)]
         slots1 = load_list(offs3, "slots1")
         factor1 = held([P, S], F32, "factor1")
         nc.sync.dma_start(factor1[:], wg1)
@@ -188,79 +185,76 @@ def tile_list_vol_surface_features_kernel(
             page = ring.tile([P, T], F32, name="page%d" % n, tag="page", bufs=3, align_bytes=64)
             nc.sync.dma_start(page[:], page1[P * n : P * (n + 1), :])
             pages.append(page)
-        load_packed_scales(d2_sc, d2_scales, nc.sync)
+        load_scales(d2_sc, d2_scales)
         d2_w = held([P, 2, N], U32, "d2_w")
         nc.sync.dma_start(d2_w[:].bitcast(I32), d2_words.rearrange("a p c i -> p a (c i)").bitcast(I32))
         slots2 = load_list(offs4, "slots2")
         factor2 = held([P, E], F32, "factor2")
         nc.sync.dma_start(factor2[:], wg2)
 
-        def gain_and_interleave(src, gain, b, dst, engine):
-            rounded = ring.tile([P, 4, src.shape[2]], BF16, name="rounded", align_bytes=64)
+        rounded = [held([P, 4, 512], BF16, "rounded%d" % i) for i in range(2)]
+        acts = [held([P, 4, 512], F32, "act%d" % i) for i in range(2)]
+        rounded2 = [a[:, 0:2, :].rearrange("p t c -> p (t c)").bitcast(BF16).rearrange("p (t c) -> p t c", t=4) for a in acts]
+        y_extra = held([P, 3, 512], F32, "y_extra")
+        z_q = [held([P, 1024], U32, "z_q%d" % i) for i in range(2)]
+        z_sc = [held([P, 1024], U8, "z_sc%d" % i) for i in range(2)]
+
+        def apply_gain(src, gain, b, dst):
             for t in range(4):
-                nc.scalar.activation(rounded[:, t, :], src[:, t, :], ACT.Copy, scale=gain[:, b, t : t + 1])
-            interleave(engine, dst, rounded[:])
+                nc.scalar.activation(dst[:, t, :], src[:, t, :], ACT.Copy, scale=gain[:, b, t : t + 1])
 
-        def z_tiles(width):
-            codes = ring.tile([P, 2 * width], U32, name="z_q", tag="z_q", align_bytes=64)
-            scales = ring.tile([P, 2 * width], U8, name="z_sc", tag="z_sc", align_bytes=64)
-            return codes, scales
-
-        def make_z1(j0, width, engine):
-            st = staged(2 * width, "z1_st")
+        def gelu_and_gain(j0, width):
+            for i in range(4):
+                nc.scalar.activation(
+                    acts[i // 2][:, 2 * (i % 2) : 2 * (i % 2) + 2, 0:width], h1[i][:, :, j0 : j0 + width], ACT.Gelu_apprx_tanh
+                )
             for b in range(2):
-                act = ring.tile([P, 4, width], F32, name="act")
-                nc.scalar.activation(act[:], h1[b][:, :, j0 : j0 + width], ACT.Gelu_apprx_tanh)
-                gain_and_interleave(act[:], gain1, b, st[:, b * width : (b + 1) * width, :], engine[b])
-            codes, scales = z_tiles(width)
-            quantize(codes[:], scales[:], st[:])
-            return codes, scales
+                apply_gain(acts[b][:, :, 0:width], gain1, b, rounded[b][:, :, 0:width])
 
-        def make_z2(engine):
-            st = staged(2 * E, "z2_st")
-            for b in range(2):
-                gain_and_interleave(picked[b][:], gain2, b, st[:, b * E : (b + 1) * E, :], engine[b])
-            codes, scales = z_tiles(E)
-            quantize(codes[:], scales[:], st[:])
-            return codes, scales
+        def weave(width, src, i, b, engine):
+            interleave(engine, stage[i][:, b * width : (b + 1) * width, :], src[b][:, :, 0:width])
 
-        def place(n, width, passes, slots, factor, last):
-            bank = psum.tile([P, width], F32, name="y_bank", tag="y_bank", bufs=4)
+        def quantize_z(width, i):
+            quantize(z_q[i][:, 0 : 2 * width], z_sc[i][:, 0 : 2 * width], stage[i][:, 0 : 2 * width, :])
+
+        def multiply(bank, passes):
             for i, (lhs, lhs_sc, rhs, rhs_sc) in enumerate(passes):
                 nc.tensor.matmul_mx(
-                    out=bank[:], lhsT=lhs, lhsT_scale=lhs_sc, rhs=rhs, rhs_scale=rhs_sc,
+                    out=bank, lhsT=lhs, lhsT_scale=lhs_sc, rhs=rhs, rhs_scale=rhs_sc,
                     start=(i == 0), stop=(i == len(passes) - 1),
                 )
-            y = ring.tile([P, width], F32, name="y", tag="y", bufs=4)
-            nc.scalar.copy(y[:], bank[:])
-            nc.vector.tensor_tensor(pages[n][:].indirect(slots), y[:], factor, ALU.mult)
-            if last:
-                nc.sync.dma_start(out[P * n : P * (n + 1), :], pages[n][:])
 
-        def place_y1(z, j0, width, last=False):
+        def place(n, bank, y, slots, factor):
+            nc.scalar.copy(y, bank)
+            nc.vector.tensor_tensor(pages[n][:].indirect(slots), y, factor, ALU.mult)
+
+        def place_y1(i, j0, width, bank0, y, blocks=range(3)):
             cols = slice(j0, j0 + width)
-            for n in range(3):
+            for n in blocks:
                 ns = slice(P * n, P * (n + 1))
                 passes = [(d1_q[:, ns].bitcast(FP8X4), d1_sc[:, ns], v_w[:, cols].bitcast(FP8X4), v_sc[:, cols])]
                 for b in range(2):
                     zs = slice(b * width, (b + 1) * width)
                     passes.append((
                         w3_w[:, b, 2 * P * n : 2 * P * (n + 1)].bitcast(FP4X4), w3_sc[:, N * b + P * n : N * b + P * (n + 1)],
-                        z[0][:, zs].bitcast(FP8X4), z[1][:, zs],
+                        z_q[i][:, zs].bitcast(FP8X4), z_sc[i][:, zs],
                     ))
-                place(n, width, passes, slots1[:, j0 // 16 : (j0 + width) // 16], factor1[:, cols], last)
+                bank = banks[bank0 + n][:, 0:width]
+                multiply(bank, passes)
+                place(n, bank, y[n][:, 0:width], slots1[:, j0 // 16 : (j0 + width) // 16], factor1[:, cols])
 
-        def place_y2(z, last=False):
-            for n in range(3):
+        def place_y2(i, bank0, y, blocks=range(3)):
+            for n in blocks:
                 ns = slice(P * n, P * (n + 1))
                 passes = []
                 for a in range(2):
-                    passes.append((d2_w[:, a, ns].bitcast(FP8X4), d2_sc[4 * a : P, ns], v2_w[:, a, :].bitcast(FP8X4), v2_sc[4 * a : P, :]))
+                    passes.append((d2_w[:, a, ns].bitcast(FP8X4), d2_sc[:, N * a + P * n : N * a + P * (n + 1)], v2_w[a][:].bitcast(FP8X4), v2_sc[a]))
                 for b in range(2):
                     ws = slice(N * b + P * n, N * b + P * (n + 1))
                     zs = slice(b * E, (b + 1) * E)
-                    passes.append((w4_q[:, ws].bitcast(FP8X4), w4_sc[:, ws], z[0][:, zs].bitcast(FP8X4), z[1][:, zs]))
-                place(n, E, passes, slots2[:], factor2[:], last)
+                    passes.append((w4_q[:, ws].bitcast(FP8X4), w4_sc[:, ws], z_q[i][:, zs].bitcast(FP8X4), z_sc[i][:, zs]))
+                multiply(banks[bank0 + n][:], passes)
+                place(n, banks[bank0 + n][:], y[n], slots2[:], factor2[:])
 
         d1_q = held([P, N], U32, "d1_q")
         d1_sc = held([P, N], U8, "d1_sc")
@@ -268,26 +262,39 @@ def tile_list_vol_surface_features_kernel(
         w4_sc = held([P, 2 * N], U8, "w4_sc")
 
         def quantize_d1(engine):
-            st = staged(N, "d1_st")
-            interleave(engine, st[:], d1_raw[:])
-            quantize(d1_q[:], d1_sc[:], st[:])
+            st = ring.tile([P, N, 4], BF16, name="d1_st", tag="dealt", bufs=1, align_bytes=64)
+            interleave(engine, st[:, 0:N, :], d1_raw[:])
+            quantize(d1_q[:], d1_sc[:], st[:, 0:N, :])
 
-        def quantize_w4(engine):
-            st = staged(2 * N, "w4_st")
+        def quantize_w4(engine, st):
             for b in range(2):
-                interleave(engine, st[:, N * b : N * (b + 1), :], w4_raw[b][:])
-                quantize(w4_q[:, N * b : N * (b + 1)], w4_sc[:, N * b : N * (b + 1)], st[:, N * b : N * (b + 1), :])
+                interleave(engine, st[b], w4_raw[b][:])
+            for b in range(2):
+                quantize(w4_q[:, N * b : N * (b + 1)], w4_sc[:, N * b : N * (b + 1)], st[b])
 
-        ss, vv, sv, vs = (nc.scalar, nc.scalar), (nc.vector, nc.vector), (nc.scalar, nc.vector), (nc.vector, nc.scalar)
-        za = make_z1(0, 256, ss)
-        quantize_d1(nc.scalar)
-        quantize_w4(nc.vector)
-        z2 = make_z2(vv)
-        place_y1(za, 0, 256)
-        zb = make_z1(256, 256, ss)
-        place_y2(z2)
-        zc = make_z1(512, 256, ss)
-        place_y1(zb, 256, 256)
-        zd = make_z1(768, 256, ss)
-        place_y1(zc, 512, 256)
-        place_y1(zd, 768, 256, last=True)
+        quantize_d1(nc.vector)
+        gelu_and_gain(0, 512)
+        for b in range(2):
+            weave(512, rounded, 1, b, nc.vector)
+        quantize_z(512, 1)
+        quantize_w4(nc.vector, [stage[1][:, 0:N, :], stage[1][:, N : 2 * N, :]])
+        for b in range(2):
+            apply_gain(picked[b][:], gain2, b, rounded2[b])
+        weave(E, rounded2, 0, 0, nc.vector)
+        place_y1(1, 0, 512, 4, [picked[1][:, n, :] for n in range(3)], [0])
+        weave(E, rounded2, 0, 1, nc.scalar)
+        quantize_z(E, 0)
+        place_y1(1, 0, 512, 4, [picked[1][:, n, :] for n in range(3)], [1, 2])
+        gelu_and_gain(512, 256)
+        for b in range(2):
+            weave(256, rounded, 1, b, nc.scalar)
+        quantize_z(256, 1)
+        place_y2(0, 0, [y_extra[:, n, :] for n in range(3)])
+        gelu_and_gain(768, 256)
+        for b in range(2):
+            weave(256, rounded, 0, b, nc.scalar)
+        quantize_z(256, 0)
+        place_y1(1, 512, 256, 4, [picked[0][:, n, :] for n in range(3)])
+        place_y1(0, 768, 256, 0, [picked[1][:, n, :] for n in range(3)])
+        for n in range(3):
+            nc.sync.dma_start(out[P * n : P * (n + 1), :], pages[n][:])

@@ -49,8 +49,8 @@ def tile_list_vol_surface_features_kernel(
                     src[:, 4 * q : 4 * q + 4, :].bitcast(I32).rearrange("a r c -> r a c"),
                 )
 
-        def load_words(src, name):
-            t = ring.tile([P, T], U32, name=name, tag="wide", bufs=3, align_bytes=64)
+        def load_words(src, name, tag):
+            t = ring.tile([P, T], U32, name=name, tag=tag, bufs=1, align_bytes=64)
             nc.sync.dma_start(t[:].bitcast(I32), src.rearrange("p t i -> p (t i)").bitcast(I32))
             return t
 
@@ -66,14 +66,17 @@ def tile_list_vol_surface_features_kernel(
         def copy_on(engine, dst, src):
             if engine is nc.scalar:
                 nc.scalar.copy(dst, src)
+            elif engine is nc.gpsimd:
+                nc.gpsimd.tensor_scalar(dst, src, 1.0, 0.0, ALU.mult, ALU.add)
             else:
                 engine.tensor_copy(dst, src)
 
         def interleave(engine, dst, src):
+            if engine is nc.gpsimd:
+                return copy_on(engine, dst, src.rearrange("p t c -> p c t"))
             copy_on(engine, dst.rearrange("p (c i) t -> p c t i", i=4), src.rearrange("p t (c i) -> p c t i", i=4))
 
-        fetched = [held([P, 4, E], F32, "fetch%d_st" % b) for b in range(2)]
-        stage = [f[:].rearrange("p t c -> p (t c)").bitcast(BF16).rearrange("p (c t) -> p c t", t=4) for f in fetched]
+        rounded = [held([P, 4, 512], BF16, "rounded%d" % i) for i in range(2)]
         banks = [psum.tile([P, 512], F32, name="bank%d" % i) for i in range(8)]
 
         def quantize(codes, scales, src):
@@ -94,36 +97,40 @@ def tile_list_vol_surface_features_kernel(
                 tab_sc[32 * q : 32 * (q + 1), :].bitcast(I32),
                 tab_scales[:, 4 * q : 4 * q + 4, :].bitcast(I32).broadcast_to([8, 4, T // 4]),
             )
-        tab_w = load_words(tab_words[0], "tab_w")
+        tab_w = load_words(tab_words[0], "tab_w", "tab_w")
         w1_raw = [load_rows(w1[:, 0:256], "w1_raw0", "raw_a")]
         w1_raw.append(load_rows(w1[:, 256:512], "w1_raw1", "raw_a"))
         central = load_list(pos1, "central")
-        w1_raw.append(load_rows(w1[:, 512:768], "w1_raw2", "first_rows", 1))
+        w1_raw.append(load_rows(w1[:, 512:768], "w1_raw2", "rows0", 1))
         load_scales(w2_sc_raw, w2_scales)
         w2_raw = held([P, 2, 2 * H], U8, "w2_raw")
         nc.sync.dma_start(w2_raw[:].bitcast(I32), w2_words.rearrange("a p c -> p a c").bitcast(I32))
-        w1_raw.append(load_rows(w1[:, 768:1024], "w1_raw3", "raw_b", 1))
+        w1_raw.append(load_rows(w1[:, 768:1024], "w1_raw3", "rows1", 1))
         idx2 = load_list(offs2, "idx2")
         load_scales(tab2_sc, tab2_scales)
-        tab2_w = [load_words(tab2_words[a], "tab2_w%d" % a) for a in range(2)]
+        tab2_w = [load_words(tab2_words[a], "tab2_w%d" % a, ("tab2_w0", "last_words")[a]) for a in range(2)]
 
         v_sc = held([P, S], U8, "v_sc")
         nc.vector.tensor_copy(v_sc[:], tab_sc[:].indirect(idx[:]))
         v_w = held([P, S], U32, "v_w")
         w1_q = [ring.tile([P, 512], U32, name="w1_q%d" % b, tag="codes%d" % b, bufs=1, align_bytes=64) for b in range(2)]
         w1_sc = [ring.tile([P, 512], U8, name="w1_sc%d" % b, tag="plane%d" % b, bufs=1, align_bytes=64) for b in range(2)]
-        h1 = [ring.tile([P, 2, S], F32, name="h1_0", tag="first_rows", bufs=1)]
-        h1 = h1 + [held([P, 2, S], F32, "h1_%d" % i) for i in range(1, 4)]
+        h1 = [ring.tile([P, 2, S], F32, name="h1_%d" % i, tag="rows%d" % i, bufs=1) for i in range(4)]
+        fetched = [held([P, 4, E], F32, "fetch0_st"), ring.tile([P, 4, E], F32, name="fetch1_st", tag="last_words", bufs=1, align_bytes=64)]
+        stage = [f[:].rearrange("p t c -> p (t c)").bitcast(BF16).rearrange("p (c t) -> p c t", t=4) for f in fetched]
         picked = [held([P, 4, E], F32, "picked%d" % b) for b in range(2)]
 
         def quantize_w1(b):
-            st = stage[b][:, 0:512, :]
+            st = rounded[b][:].rearrange("p t c -> p (t c)").rearrange("p (c t) -> p c t", t=4)
             for u in range(2):
                 nc.scalar.copy(
                     st.rearrange("p (t m) j -> p m j t", t=4)[:, 64 * u : 64 * (u + 1)],
                     w1_raw[2 * b + u][:].rearrange("p j (m t) -> p m j t", t=4),
                 )
             quantize(w1_q[b][:], w1_sc[b][:], st)
+
+        def pick(b, t):
+            nc.vector.tensor_copy(fetched[b][:, t, :], h1[2 * b + t // 2][:, t % 2, :].indirect(central[:]))
 
         nc.vector.tensor_copy(v_w[:], tab_w[:].indirect(idx[:]))
         quantize_w1(0)
@@ -138,7 +145,8 @@ def tile_list_vol_surface_features_kernel(
                         rhs=v_w[:, cols].bitcast(FP8X4), rhs_scale=v_sc[:, cols], start=True, stop=True,
                     )
                     nc.scalar.copy(h1[2 * b + t // 2][:, t % 2, cols], bank[:])
-                nc.vector.tensor_copy(fetched[b][:, t, :], h1[2 * b + t // 2][:, t % 2, :].indirect(central[:]))
+                if b == 0:
+                    pick(0, t)
 
         v2_w = [ring.tile([P, E], U32, name="v2_w%d" % a, tag="codes%d" % a, bufs=1, align_bytes=64) for a in range(2)]
         w2_w = ring.tile([P, 2, 2 * H], U8, name="w2_w", tag="dealt", bufs=1, align_bytes=64)
@@ -156,15 +164,17 @@ def tile_list_vol_surface_features_kernel(
             w2_raw[:].rearrange("p a c -> p (a c)").bitcast(U16).rearrange("p (b m t) -> p b t m", t=4, m=P),
         )
         nc.vector.tensor_copy(v2_w[1][:], tab2_w[1][:].indirect(idx2[:]))
+        for t in range(4):
+            pick(1, t)
         for b in range(2):
             for t in range(4):
                 r0 = 512 * b + P * t
-                bank = banks[t]
-                for a in range(2):
+                bank = banks[4 * (1 - b) + t]
+                for a in (1, 0):
                     nc.tensor.matmul_mx(
                         out=bank[:], lhsT=w2_w[:, a, 2 * r0 : 2 * (r0 + P)].bitcast(FP4X4),
                         lhsT_scale=w2_sc[:, H * a + r0 : H * a + r0 + P],
-                        rhs=v2_w[a][:].bitcast(FP8X4), rhs_scale=v2_sc[a], start=(a == 0), stop=(a == 1),
+                        rhs=v2_w[a][:].bitcast(FP8X4), rhs_scale=v2_sc[a], start=(a == 1), stop=(a == 0),
                     )
                 nc.vector.tensor_tensor(picked[b][:, t, :], bank[:], fetched[b][:, t, :], ALU.min)
 
@@ -192,7 +202,6 @@ def tile_list_vol_surface_features_kernel(
         factor2 = held([P, E], F32, "factor2")
         nc.sync.dma_start(factor2[:], wg2)
 
-        rounded = [held([P, 4, 512], BF16, "rounded%d" % i) for i in range(2)]
         acts = [held([P, 4, 512], F32, "act%d" % i) for i in range(2)]
         rounded2 = [a[:, 0:2, :].rearrange("p t c -> p (t c)").bitcast(BF16).rearrange("p (t c) -> p t c", t=4) for a in acts]
         y_extra = held([P, 3, 512], F32, "y_extra")
@@ -256,13 +265,14 @@ def tile_list_vol_surface_features_kernel(
                 multiply(banks[bank0 + n][:], passes)
                 place(n, banks[bank0 + n][:], y[n], slots2[:], factor2[:])
 
+        w4_st = held([P, 2 * N, 4], BF16, "w4_st")
         d1_q = held([P, N], U32, "d1_q")
         d1_sc = held([P, N], U8, "d1_sc")
         w4_q = held([P, 2 * N], U32, "w4_q")
         w4_sc = held([P, 2 * N], U8, "w4_sc")
 
         def quantize_d1(engine):
-            st = ring.tile([P, N, 4], BF16, name="d1_st", tag="dealt", bufs=1, align_bytes=64)
+            st = ring.tile([P, N, 4], BF16, name="d1_st", tag="d1_st", bufs=1, align_bytes=64)
             interleave(engine, st[:, 0:N, :], d1_raw[:])
             quantize(d1_q[:], d1_sc[:], st[:, 0:N, :])
 
@@ -272,12 +282,12 @@ def tile_list_vol_surface_features_kernel(
             for b in range(2):
                 quantize(w4_q[:, N * b : N * (b + 1)], w4_sc[:, N * b : N * (b + 1)], st[b])
 
-        quantize_d1(nc.vector)
+        quantize_d1(nc.gpsimd)
         gelu_and_gain(0, 512)
         for b in range(2):
             weave(512, rounded, 1, b, nc.vector)
         quantize_z(512, 1)
-        quantize_w4(nc.vector, [stage[1][:, 0:N, :], stage[1][:, N : 2 * N, :]])
+        quantize_w4(nc.gpsimd, [w4_st[:, 0:N, :], w4_st[:, N : 2 * N, :]])
         for b in range(2):
             apply_gain(picked[b][:], gain2, b, rounded2[b])
         weave(E, rounded2, 0, 0, nc.vector)

@@ -100,9 +100,9 @@ def tile_list_vol_surface_features_kernel(
         tab_w = load_words(tab_words[0], "tab_w", "tab_w")
         w1_raw = [load_rows(w1[:, 0:256], "w1_raw0", "raw_a")]
         w1_raw.append(load_rows(w1[:, 256:512], "w1_raw1", "raw_a"))
+        load_scales(w2_sc_raw, w2_scales)
         central = load_list(pos1, "central")
         w1_raw.append(load_rows(w1[:, 512:768], "w1_raw2", "rows0", 1))
-        load_scales(w2_sc_raw, w2_scales)
         w2_raw = held([P, 2, 2 * H], U8, "w2_raw")
         nc.sync.dma_start(w2_raw[:].bitcast(I32), w2_words.rearrange("a p c -> p a c").bitcast(I32))
         w1_raw.append(load_rows(w1[:, 768:1024], "w1_raw3", "rows1", 1))
@@ -121,12 +121,19 @@ def tile_list_vol_surface_features_kernel(
         picked = [held([P, 4, E], F32, "picked%d" % b) for b in range(2)]
 
         def quantize_w1(b):
-            st = rounded[b][:].rearrange("p t c -> p (t c)").rearrange("p (c t) -> p c t", t=4)
+            st = ring.tile([P, 512, 4], BF16, name="w1_%d_st" % b, tag="w1_st%d" % b, bufs=1, align_bytes=64)[:]
             for u in range(2):
-                nc.scalar.copy(
-                    st.rearrange("p (t m) j -> p m j t", t=4)[:, 64 * u : 64 * (u + 1)],
-                    w1_raw[2 * b + u][:].rearrange("p j (m t) -> p m j t", t=4),
-                )
+                if 2 * b + u < 3:
+                    nc.scalar.copy(
+                        st.rearrange("p (t m) j -> p m j t", t=4)[:, 64 * u : 64 * (u + 1)],
+                        w1_raw[2 * b + u][:].rearrange("p j (m t) -> p m j t", t=4),
+                    )
+                else:
+                    copy_on(
+                        nc.gpsimd,
+                        st.rearrange("p (t m) j -> p t m j", t=4)[:, :, 64 * u : 64 * (u + 1)],
+                        w1_raw[2 * b + u][:].rearrange("p j (m t) -> p t m j", t=4),
+                    )
             quantize(w1_q[b][:], w1_sc[b][:], st)
 
         def pick(b, t):
@@ -151,7 +158,7 @@ def tile_list_vol_surface_features_kernel(
         v2_w = [ring.tile([P, E], U32, name="v2_w%d" % a, tag="codes%d" % a, bufs=1, align_bytes=64) for a in range(2)]
         w2_w = ring.tile([P, 2, 2 * H], U8, name="w2_w", tag="dealt", bufs=1, align_bytes=64)
         w2_sc = held([P, 2 * H], U8, "w2_sc")
-        v2_planes = ring.tile([P, 2, E], U8, name="v2_planes", tag="plane0", bufs=1, align_bytes=64)
+        v2_planes = ring.tile([P, 2, E], U8, name="v2_planes", tag="w1_st1", bufs=1, align_bytes=64)
         v2_sc = [v2_planes[:, a, :] for a in range(2)]
         for a in range(2):
             nc.vector.tensor_copy(v2_sc[a], tab2_sc[:, T * a : T * (a + 1)].indirect(idx2[:]))
@@ -178,15 +185,15 @@ def tile_list_vol_surface_features_kernel(
                     )
                 nc.vector.tensor_tensor(picked[b][:, t, :], bank[:], fetched[b][:, t, :], ALU.min)
 
+        d1_raw = load_rows(d1, "d1_raw", "raw_a")
+        w4_raw = [load_rows(w4[512 * b : 512 * (b + 1), :], "w4_raw%d" % b, ("raw_a", "raw_b")[b], 2 - b) for b in range(2)]
         gain1 = held([P, 2, 4], F32, "gain1")
         nc.sync.dma_start(gain1[:], g1.rearrange("(b p t) -> p b t", b=2, t=4))
         gain2 = held([P, 2, 4], F32, "gain2")
         nc.sync.dma_start(gain2[:], g2.rearrange("(b p t) -> p b t", b=2, t=4))
-        d1_raw = load_rows(d1, "d1_raw", "raw_a")
         w3_w = held([P, 2, 2 * N], U8, "w3_w")
         nc.sync.dma_start(w3_w[:].bitcast(I32), w3_words.rearrange("a p c -> p a c").bitcast(I32))
         load_scales(w3_sc, w3_scales)
-        w4_raw = [load_rows(w4[512 * b : 512 * (b + 1), :], "w4_raw%d" % b, ("raw_a", "raw_b")[b], 2 - b) for b in range(2)]
         slots1 = load_list(offs3, "slots1")
         factor1 = held([P, S], F32, "factor1")
         nc.sync.dma_start(factor1[:], wg1)
@@ -212,11 +219,14 @@ def tile_list_vol_surface_features_kernel(
             for t in range(4):
                 nc.scalar.activation(dst[:, t, :], src[:, t, :], ACT.Copy, scale=gain[:, b, t : t + 1])
 
-        def gelu_and_gain(j0, width):
+        def gelu(j0, width):
             for i in range(4):
                 nc.scalar.activation(
                     acts[i // 2][:, 2 * (i % 2) : 2 * (i % 2) + 2, 0:width], h1[i][:, :, j0 : j0 + width], ACT.Gelu_apprx_tanh
                 )
+
+        def gelu_and_gain(j0, width):
+            gelu(j0, width)
             for b in range(2):
                 apply_gain(acts[b][:, :, 0:width], gain1, b, rounded[b][:, :, 0:width])
 
@@ -284,27 +294,31 @@ def tile_list_vol_surface_features_kernel(
 
         quantize_d1(nc.gpsimd)
         gelu_and_gain(0, 512)
-        for b in range(2):
-            weave(512, rounded, 1, b, nc.vector)
-        quantize_z(512, 1)
+        first_half = y_extra[:, 0:2, :].rearrange("p n c -> p (n c)").bitcast(BF16).rearrange("p (c t) -> p c t", t=4)
+        interleave(nc.gpsimd, first_half, rounded[0][:])
+        second_half = ring.tile([P, 512, 4], BF16, name="second_half", tag="w1_st0", bufs=1, align_bytes=64)
+        interleave(nc.gpsimd, second_half[:], rounded[1][:])
+        quantize(z_q[1][:, 0:512], z_sc[1][:, 0:512], first_half)
+        quantize(z_q[1][:, 512:1024], z_sc[1][:, 512:1024], second_half[:])
         quantize_w4(nc.gpsimd, [w4_st[:, 0:N, :], w4_st[:, N : 2 * N, :]])
         for b in range(2):
             apply_gain(picked[b][:], gain2, b, rounded2[b])
-        weave(E, rounded2, 0, 0, nc.vector)
-        place_y1(1, 0, 512, 4, [picked[1][:, n, :] for n in range(3)], [0])
+        interleave(nc.vector, second_half[:], rounded2[0])
         weave(E, rounded2, 0, 1, nc.scalar)
-        quantize_z(E, 0)
-        place_y1(1, 0, 512, 4, [picked[1][:, n, :] for n in range(3)], [1, 2])
-        gelu_and_gain(512, 256)
-        for b in range(2):
-            weave(256, rounded, 1, b, nc.scalar)
-        quantize_z(256, 1)
-        place_y2(0, 0, [y_extra[:, n, :] for n in range(3)])
-        gelu_and_gain(768, 256)
-        for b in range(2):
-            weave(256, rounded, 0, b, nc.scalar)
-        quantize_z(256, 0)
-        place_y1(1, 512, 256, 4, [picked[0][:, n, :] for n in range(3)])
-        place_y1(0, 768, 256, 0, [picked[1][:, n, :] for n in range(3)])
+        quantize(z_q[0][:, 0:E], z_sc[0][:, 0:E], second_half[:])
+        quantize(z_q[0][:, E : 2 * E], z_sc[0][:, E : 2 * E], stage[0][:, E : 2 * E, :])
+        place_y1(1, 0, 512, 4, [picked[1][:, n, :] for n in range(3)])
+        y2 = [y_extra[:, 0, :], y_extra[:, 1, :], rounded[1][:, 0:2, :].rearrange("p t c -> p (t c)").bitcast(F32)]
+        gelu(512, 512)
+        place_y2(0, 0, y2, [0])
+        apply_gain(acts[0][:], gain1, 0, rounded[0][:])
+        weave(512, rounded, 1, 0, nc.scalar)
+        quantize(z_q[1][:, 0:512], z_sc[1][:, 0:512], stage[1][:, 0:512, :])
+        place_y2(0, 0, y2, [1])
+        apply_gain(acts[1][:], gain1, 1, rounded[1][:])
+        weave(512, rounded, 1, 1, nc.scalar)
+        quantize(z_q[1][:, 512:1024], z_sc[1][:, 512:1024], stage[1][:, 512:1024, :])
+        place_y2(0, 0, y2, [2])
+        place_y1(1, 512, 512, 4, [picked[0][:, n, :] for n in range(3)])
         for n in range(3):
             nc.sync.dma_start(out[P * n : P * (n + 1), :], pages[n][:])

from contextlib import ExitStack

import concourse.mybir as mybir

K, M, H, N, T, S, E = 512, 1024, 1024, 384, 2048, 1024, 512
FLOPS = 4160749568

F32 = mybir.dt.float32
BF16 = mybir.dt.bfloat16
I32 = mybir.dt.int32
U32 = mybir.dt.uint32
U16 = mybir.dt.uint16
U8 = mybir.dt.uint8
FP8X4 = mybir.dt.float8_e4m3fn_x4
FP4X4 = mybir.dt.float4_e2m1fn_x4
ACT = mybir.ActivationFunctionType
ALU = mybir.AluOpType

P = 128


def tile_list_vol_surface_features_kernel(
    tc, tab_words, tab_scales, tab2_words, tab2_scales, offs, offs2, pos1, offs3, offs4, w1, d1,
    w2_words, w2_scales, d2_words, d2_scales, w3_words, w3_scales, w4, g1, g2, wg1, wg2, page1, out,
):
    nc = tc.nc
    with ExitStack() as ctx:
        keep = ctx.enter_context(tc.tile_pool(name="keep", bufs=1))
        ring = ctx.enter_context(tc.tile_pool(name="ring", bufs=2))
        psum = ctx.enter_context(tc.psum_pool(name="psum", bufs=1))

        def held(shape, dtype, name):
            return keep.tile(shape, dtype, name=name, align_bytes=64)

        def load_list(src, name):
            t = keep.tile(list(src.shape), U16, name=name)
            nc.sync.dma_start(t[:], src)
            return t

        def zeroed(width, name, engine):
            t = held([P, width], U8, name)
            engine.memset(t[:].bitcast(I32), 0)
            return t

        def load_scales(t, src):
            for q in range(4):
                nc.sync.dma_start(
                    t[32 * q : 32 * q + 4, :].bitcast(I32).rearrange("r (a c) -> r a c", a=2),
                    src[:, 4 * q : 4 * q + 4, :].bitcast(I32).rearrange("a r c -> r a c"),
                )

        def load_words(src, name, tag):
            t = ring.tile([P, T], U32, name=name, tag=tag, bufs=1, align_bytes=64)
            nc.sync.dma_start(t[:].bitcast(I32), src.rearrange("p t i -> p (t i)").bitcast(I32))
            return t

        def load_rows(src, name, tag, bufs=2):
            t = ring.tile([P, 4, src.shape[1]], F32, name=name, tag=tag, bufs=bufs)
            nc.sync.dma_start(t[:], src.rearrange("(p j) c -> p j c", j=4))
            return t

        def raise_second_plane(dst, src):
            for q in range(4):
                nc.sync.dma_start(dst[32 * q : 32 * q + 4, :].bitcast(I32), src[32 * q + 4 : 32 * q + 8, :].bitcast(I32))

        def copy_on(engine, dst, src):
            if engine is nc.scalar:
                nc.scalar.copy(dst, src)
            elif engine is nc.gpsimd:
                nc.gpsimd.tensor_scalar(dst, src, 1.0, 0.0, ALU.mult, ALU.add)
            else:
                engine.tensor_copy(dst, src)

        def interleave(engine, dst, src):
            if engine is nc.gpsimd:
                return copy_on(engine, dst, src.rearrange("p t c -> p c t"))
            copy_on(engine, dst.rearrange("p (c i) t -> p c t i", i=4), src.rearrange("p t (c i) -> p c t i", i=4))

        rounded = [held([P, 4, 512], BF16, "rounded%d" % i) for i in range(2)]
        banks = [psum.tile([P, 512], F32, name="bank%d" % i) for i in range(8)]

        def quantize(codes, scales, src):
            nc.vector.quantize_mx(out=codes.bitcast(FP8X4), scales=scales, in_=src.rearrange("p c t -> p (c t)"))

        warm = held([P, 1], F32, "warm")
        nc.gpsimd.memset(warm[:], 0.0)
        warmed = held([P, 1], F32, "warmed")
        nc.scalar.activation(warmed[:], warm[:], ACT.Gelu_apprx_tanh)
        w2_sc_raw = zeroed(2 * H, "w2_sc_raw", nc.vector)
        tab2_sc = zeroed(2 * T, "tab2_sc", nc.vector)
        w3_sc = zeroed(2 * N, "w3_sc", nc.gpsimd)
        d2_sc = zeroed(2 * N, "d2_sc", nc.gpsimd)
        idx = load_list(offs, "idx")
        tab_sc = held([P, T], U8, "tab_sc")
        for q in range(4):
            nc.sync.dma_start(
                tab_sc[32 * q : 32 * (q + 1), :].bitcast(I32),
                tab_scales[:, 4 * q : 4 * q + 4, :].bitcast(I32).broadcast_to([8, 4, T // 4]),
            )
        tab_w = load_words(tab_words[0], "tab_w", "tab_w")
        w1_raw = [load_rows(w1[:, 0:256], "w1_raw0", "raw_a")]
        w1_raw.append(load_rows(w1[:, 256:512], "w1_raw1", "raw_a"))
        load_scales(w2_sc_raw, w2_scales)
        central = load_list(pos1, "central")
        w1_raw.append(load_rows(w1[:, 512:768], "w1_raw2", "rows0", 1))
        w2_raw = held([P, 2, 2 * H], U8, "w2_raw")
        nc.sync.dma_start(w2_raw[:].bitcast(I32), w2_words.rearrange("a p c -> p a c").bitcast(I32))
        w1_raw.append(load_rows(w1[:, 768:1024], "w1_raw3", "rows1", 1))
        idx2 = load_list(offs2, "idx2")
        load_scales(tab2_sc, tab2_scales)
        tab2_w = [load_words(tab2_words[a], "tab2_w%d" % a, ("tab2_w0", "last_words")[a]) for a in range(2)]

        v_sc = held([P, S], U8, "v_sc")
        nc.vector.tensor_copy(v_sc[:], tab_sc[:].indirect(idx[:]))
        v_w = held([P, S], U32, "v_w")
        w1_q = [ring.tile([P, 512], U32, name="w1_q%d" % b, tag="codes%d" % b, bufs=1, align_bytes=64) for b in range(2)]
        w1_sc = [ring.tile([P, 512], U8, name="w1_sc%d" % b, tag="plane%d" % b, bufs=1, align_bytes=64) for b in range(2)]
        h1 = [ring.tile([P, 2, S], F32, name="h1_%d" % i, tag="rows%d" % i, bufs=1) for i in range(4)]
        fetched = [held([P, 4, E], F32, "fetch0_st"), ring.tile([P, 4, E], F32, name="fetch1_st", tag="last_words", bufs=1, align_bytes=64)]
        stage = [f[:].rearrange("p t c -> p (t c)").bitcast(BF16).rearrange("p (c t) -> p c t", t=4) for f in fetched]
        picked = [held([P, 4, E], F32, "picked%d" % b) for b in range(2)]

        def quantize_w1(b):
            st = ring.tile([P, 512, 4], BF16, name="w1_%d_st" % b, tag="w1_st%d" % b, bufs=1, align_bytes=64)[:]
            for u in range(2):
                if 2 * b + u < 3:
                    nc.scalar.copy(
                        st.rearrange("p (t m) j -> p m j t", t=4)[:, 64 * u : 64 * (u + 1)],
                        w1_raw[2 * b + u][:].rearrange("p j (m t) -> p m j t", t=4),
                    )
                else:
                    copy_on(
                        nc.gpsimd,
                        st.rearrange("p (t m) j -> p t m j", t=4)[:, :, 64 * u : 64 * (u + 1)],
                        w1_raw[2 * b + u][:].rearrange("p j (m t) -> p t m j", t=4),
                    )
            quantize(w1_q[b][:], w1_sc[b][:], st)

        def pick(b, t):
            nc.vector.tensor_copy(fetched[b][:, t, :], h1[2 * b + t // 2][:, t % 2, :].indirect(central[:]))

        nc.vector.tensor_copy(v_w[:], tab_w[:].indirect(idx[:]))
        quantize_w1(0)
        quantize_w1(1)
        for b in range(2):
            for t in range(4):
                for half in range(2):
                    cols = slice(512 * half, 512 * (half + 1))
                    bank = banks[(2 * t + half) % 4]
                    nc.tensor.matmul_mx(
                        out=bank[:], lhsT=w1_q[b][:, P * t : P * (t + 1)].bitcast(FP8X4), lhsT_scale=w1_sc[b][:, P * t : P * (t + 1)],
                        rhs=v_w[:, cols].bitcast(FP8X4), rhs_scale=v_sc[:, cols], start=True, stop=True,
                    )
                    nc.scalar.copy(h1[2 * b + t // 2][:, t % 2, cols], bank[:])
                if b == 0:
                    pick(0, t)

        v2_w = [ring.tile([P, E], U32, name="v2_w%d" % a, tag="codes%d" % a, bufs=1, align_bytes=64) for a in range(2)]
        w2_w = ring.tile([P, 2, 2 * H], U8, name="w2_w", tag="dealt", bufs=1, align_bytes=64)
        w2_sc = held([P, 2 * H], U8, "w2_sc")
        v2_planes = ring.tile([P, 2, E], U8, name="v2_planes", tag="w1_st1", bufs=1, align_bytes=64)
        v2_sc = [v2_planes[:, a, :] for a in range(2)]
        for a in range(2):
            nc.vector.tensor_copy(v2_sc[a], tab2_sc[:, T * a : T * (a + 1)].indirect(idx2[:]))
        nc.vector.tensor_copy(v2_w[0][:], tab2_w[0][:].indirect(idx2[:]))
        nc.vector.tensor_copy(
            w2_sc[:].rearrange("p (b t m) -> p b t m", t=4, m=P), w2_sc_raw[:].rearrange("p (b m t) -> p b t m", t=4, m=P)
        )
        nc.vector.tensor_copy(
            w2_w[:].rearrange("p a c -> p (a c)").bitcast(U16).rearrange("p (b t m) -> p b t m", t=4, m=P),
            w2_raw[:].rearrange("p a c -> p (a c)").bitcast(U16).rearrange("p (b m t) -> p b t m", t=4, m=P),
        )
        nc.vector.tensor_copy(v2_w[1][:], tab2_w[1][:].indirect(idx2[:]))
        for t in range(4):
            pick(1, t)
        for b in range(2):
            for t in range(4):
                r0 = 512 * b + P * t
                bank = banks[4 * (1 - b) + t]
                for a in (1, 0):
                    nc.tensor.matmul_mx(
                        out=bank[:], lhsT=w2_w[:, a, 2 * r0 : 2 * (r0 + P)].bitcast(FP4X4),
                        lhsT_scale=w2_sc[:, H * a + r0 : H * a + r0 + P],
                        rhs=v2_w[a][:].bitcast(FP8X4), rhs_scale=v2_sc[a], start=(a == 1), stop=(a == 0),
                    )
                nc.vector.tensor_tensor(picked[b][:, t, :], bank[:], fetched[b][:, t, :], ALU.min)

        d1_raw = load_rows(d1, "d1_raw", "raw_a")
        w4_raw = [load_rows(w4[512 * b : 512 * (b + 1), :], "w4_raw%d" % b, ("raw_a", "raw_b")[b], 2 - b) for b in range(2)]
        gain1 = held([P, 2, 4], F32, "gain1")
        nc.sync.dma_start(gain1[:], g1.rearrange("(b p t) -> p b t", b=2, t=4))
        gain2 = held([P, 2, 4], F32, "gain2")
        nc.sync.dma_start(gain2[:], g2.rearrange("(b p t) -> p b t", b=2, t=4))
        w3_w = held([P, 2, 2 * N], U8, "w3_w")
        nc.sync.dma_start(w3_w[:].bitcast(I32), w3_words.rearrange("a p c -> p a c").bitcast(I32))
        load_scales(w3_sc, w3_scales)
        slots1 = load_list(offs3, "slots1")
        factor1 = held([P, S], F32, "factor1")
        nc.sync.dma_start(factor1[:], wg1)
        pages = []
        for n in range(3):
            page = ring.tile([P, T], F32, name="page%d" % n, tag="page", bufs=3, align_bytes=64)
            nc.sync.dma_start(page[:], page1[P * n : P * (n + 1), :])
            pages.append(page)
        load_scales(d2_sc, d2_scales)
        d2_w = held([P, 2, N], U32, "d2_w")
        nc.sync.dma_start(d2_w[:].bitcast(I32), d2_words.rearrange("a p c i -> p a (c i)").bitcast(I32))
        slots2 = load_list(offs4, "slots2")
        factor2 = held([P, E], F32, "factor2")
        nc.sync.dma_start(factor2[:], wg2)

        acts = [held([P, 4, 512], F32, "act%d" % i) for i in range(2)]
        rounded2 = [a[:, 0:2, :].rearrange("p t c -> p (t c)").bitcast(BF16).rearrange("p (t c) -> p t c", t=4) for a in acts]
        y_extra = held([P, 3, 512], F32, "y_extra")
        z_q = [held([P, 1024], U32, "z_q%d" % i) for i in range(2)]
        z_sc = [held([P, 1024], U8, "z_sc%d" % i) for i in range(2)]

        def apply_gain(src, gain, b, dst):
            for t in range(4):
                nc.scalar.activation(dst[:, t, :], src[:, t, :], ACT.Copy, scale=gain[:, b, t : t + 1])

        def gelu(j0, width):
            for i in range(4):
                nc.scalar.activation(
                    acts[i // 2][:, 2 * (i % 2) : 2 * (i % 2) + 2, 0:width], h1[i][:, :, j0 : j0 + width], ACT.Gelu_apprx_tanh
                )

        def gelu_and_gain(j0, width):
            gelu(j0, width)
            for b in range(2):
                apply_gain(acts[b][:, :, 0:width], gain1, b, rounded[b][:, :, 0:width])

        def weave(width, src, i, b, engine):
            interleave(engine, stage[i][:, b * width : (b + 1) * width, :], src[b][:, :, 0:width])

        def quantize_z(width, i):
            quantize(z_q[i][:, 0 : 2 * width], z_sc[i][:, 0 : 2 * width], stage[i][:, 0 : 2 * width, :])

        def multiply(bank, passes):
            for i, (lhs, lhs_sc, rhs, rhs_sc) in enumerate(passes):
                nc.tensor.matmul_mx(
                    out=bank, lhsT=lhs, lhsT_scale=lhs_sc, rhs=rhs, rhs_scale=rhs_sc,
                    start=(i == 0), stop=(i == len(passes) - 1),
                )

        def place(n, bank, y, slots, factor):
            nc.scalar.copy(y, bank)
            nc.vector.tensor_tensor(pages[n][:].indirect(slots), y, factor, ALU.mult)

        def place_y1(i, j0, width, bank0, y, blocks=range(3)):
            cols = slice(j0, j0 + width)
            for n in blocks:
                ns = slice(P * n, P * (n + 1))
                passes = [(d1_q[:, ns].bitcast(FP8X4), d1_sc[:, ns], v_w[:, cols].bitcast(FP8X4), v_sc[:, cols])]
                for b in range(2):
                    zs = slice(b * width, (b + 1) * width)
                    passes.append((
                        w3_w[:, b, 2 * P * n : 2 * P * (n + 1)].bitcast(FP4X4), w3_sc[:, N * b + P * n : N * b + P * (n + 1)],
                        z_q[i][:, zs].bitcast(FP8X4), z_sc[i][:, zs],
                    ))
                bank = banks[bank0 + n][:, 0:width]
                multiply(bank, passes)
                place(n, bank, y[n][:, 0:width], slots1[:, j0 // 16 : (j0 + width) // 16], factor1[:, cols])

        def place_y2(i, bank0, y, blocks=range(3)):
            for n in blocks:
                ns = slice(P * n, P * (n + 1))
                passes = []
                for a in range(2):
                    passes.append((d2_w[:, a, ns].bitcast(FP8X4), d2_sc[:, N * a + P * n : N * a + P * (n + 1)], v2_w[a][:].bitcast(FP8X4), v2_sc[a]))
                for b in range(2):
                    ws = slice(N * b + P * n, N * b + P * (n + 1))
                    zs = slice(b * E, (b + 1) * E)
                    passes.append((w4_q[:, ws].bitcast(FP8X4), w4_sc[:, ws], z_q[i][:, zs].bitcast(FP8X4), z_sc[i][:, zs]))
                multiply(banks[bank0 + n][:], passes)
                place(n, banks[bank0 + n][:], y[n], slots2[:], factor2[:])

        w4_st = held([P, 2 * N, 4], BF16, "w4_st")
        d1_q = held([P, N], U32, "d1_q")
        d1_sc = held([P, N], U8, "d1_sc")
        w4_q = held([P, 2 * N], U32, "w4_q")
        w4_sc = held([P, 2 * N], U8, "w4_sc")

        def quantize_d1(engine):
            st = ring.tile([P, N, 4], BF16, name="d1_st", tag="d1_st", bufs=1, align_bytes=64)
            interleave(engine, st[:, 0:N, :], d1_raw[:])
            quantize(d1_q[:], d1_sc[:], st[:, 0:N, :])

        def quantize_w4(engine, st):
            for b in range(2):
                interleave(engine, st[b], w4_raw[b][:])
            for b in range(2):
                quantize(w4_q[:, N * b : N * (b + 1)], w4_sc[:, N * b : N * (b + 1)], st[b])

        quantize_d1(nc.gpsimd)
        gelu_and_gain(0, 512)
        first_half = y_extra[:, 0:2, :].rearrange("p n c -> p (n c)").bitcast(BF16).rearrange("p (c t) -> p c t", t=4)
        interleave(nc.gpsimd, first_half, rounded[0][:])
        second_half = ring.tile([P, 512, 4], BF16, name="second_half", tag="w1_st0", bufs=1, align_bytes=64)
        interleave(nc.gpsimd, second_half[:], rounded[1][:])
        quantize(z_q[1][:, 0:512], z_sc[1][:, 0:512], first_half)
        quantize(z_q[1][:, 512:1024], z_sc[1][:, 512:1024], second_half[:])
        quantize_w4(nc.gpsimd, [w4_st[:, 0:N, :], w4_st[:, N : 2 * N, :]])
        for b in range(2):
            apply_gain(picked[b][:], gain2, b, rounded2[b])
        interleave(nc.vector, second_half[:], rounded2[0])
        weave(E, rounded2, 0, 1, nc.scalar)
        quantize(z_q[0][:, 0:E], z_sc[0][:, 0:E], second_half[:])
        quantize(z_q[0][:, E : 2 * E], z_sc[0][:, E : 2 * E], stage[0][:, E : 2 * E, :])
        place_y1(1, 0, 512, 4, [picked[1][:, n, :] for n in range(3)])
        y2 = [y_extra[:, 0, :], y_extra[:, 1, :], rounded[1][:, 0:2, :].rearrange("p t c -> p (t c)").bitcast(F32)]
        gelu(512, 512)
        place_y2(0, 0, y2, [0])
        apply_gain(acts[0][:], gain1, 0, rounded[0][:])
        weave(512, rounded, 1, 0, nc.scalar)
        quantize(z_q[1][:, 0:512], z_sc[1][:, 0:512], stage[1][:, 0:512, :])
        place_y2(0, 0, y2, [1])
        apply_gain(acts[1][:], gain1, 1, rounded[1][:])
        weave(512, rounded, 1, 1, nc.scalar)
        quantize(z_q[1][:, 512:1024], z_sc[1][:, 512:1024], stage[1][:, 512:1024, :])
        place_y2(0, 0, y2, [2])
        place_y1(1, 512, 512, 4, [picked[0][:, n, :] for n in range(3)])
        for n in range(3):
            nc.sync.dma_start(out[P * n : P * (n + 1), :], pages[n][:])
